import numpy as np
import ml_dtypes


def mxq(x, axis, fmt="e4m3"):
    dtype, down = {"e4m3": (ml_dtypes.float8_e4m3fn, 7), "e5m2": (ml_dtypes.float8_e5m2, 14)}[fmt]
    v = np.moveaxis(np.asarray(x, np.float32).astype(ml_dtypes.bfloat16).astype(np.float64), axis, -1)
    blocks = v.reshape(v.shape[:-1] + (-1, 32))
    amax = np.abs(blocks).max(-1, keepdims=True)
    byte = np.maximum(np.where(amax > 0, np.frexp(amax)[1] - 1 + 127, 0) - down, 1)
    scale = np.exp2(byte - 127.0)
    codes = (blocks / scale).astype(np.float32).astype(dtype).astype(np.float64)
    return np.moveaxis((codes * scale).reshape(v.shape), -1, axis)


WIDE = False


def mx_kscale(k):
    if not WIDE:
        return np.ones(k)
    levels = np.array([10, -10, 5, -5, 0])
    if k % 512:
        return np.exp2(np.random.permutation(np.resize(levels, k // 32))).repeat(32)
    a = np.empty((k // 512, 16))
    for p in range(k // 512):
        a[p, :8] = np.random.permutation(np.resize(levels, 8))
        for g in range(8):
            far = levels[np.abs(levels - a[p, g]) >= 10]
            a[p, g + 8] = far[np.random.randint(len(far))]
    return np.exp2(a.ravel()).repeat(32)


def f64(x):
    return np.asarray(x).astype(np.float64)


def striped(idx):
    return np.tile(np.asarray(idx).reshape(-1, 16).T, (8, 1)).astype(np.uint16)


def unstriped(offs):
    return offs[:16].T.reshape(-1).astype(np.int64)


def striped8(idx):
    return np.asarray(idx).reshape(8, -1, 16).transpose(0, 2, 1).reshape(128, -1).astype(np.uint16)


def unstriped8(offs):
    return offs.reshape(8, 16, -1).transpose(0, 2, 1).reshape(8, -1).astype(np.int64)


def pick8(x, idx, run):
    r = np.arange(len(x))
    return x[r[:, None], idx[r % (8 * run) // run]]


E2M1 = np.array([0.0, 0.5, 1.0, 1.5, 2.0, 3.0, 4.0, 6.0, -0.0, -0.5, -1.0, -1.5, -2.0, -3.0, -4.0, -6.0])


def pack_weight(w, fmt):
    k, n = w.shape
    w = f64(np.asarray(w, np.float32).astype(ml_dtypes.bfloat16)).reshape(k // 32, 32, n)
    amax = np.abs(w).max(1)
    if fmt == "e4m3":
        byte = np.frexp(amax)[1] - 1 + 127 - 7
    else:
        mant, ex = np.frexp(amax / 6.0)
        byte = np.where(mant > 0.5, ex, ex - 1) + 127
    byte = np.clip(np.where(amax > 0, byte, 1), 1, 254)
    scaled = (w * np.exp2(127.0 - byte)[:, None, :]).reshape(k, n).astype(np.float32)
    by_word = np.ascontiguousarray(scaled.reshape(k // 512, 128, 4, n).transpose(0, 1, 3, 2))
    if fmt == "e4m3":
        words = by_word.astype(ml_dtypes.float8_e4m3fn).view(np.uint8)
    else:
        c = by_word.astype(ml_dtypes.float4_e2m1fn).view(np.uint8) & 0xF
        words = (c[..., 0::2] | (c[..., 1::2] << 4)).reshape(k // 512, 128, 2 * n)
    return np.ascontiguousarray(words), np.ascontiguousarray(byte.astype(np.uint8).reshape(k // 512, 16, n))


def unpack_weight(words, scales, fmt):
    g, _, n = scales.shape
    words = np.ascontiguousarray(words).reshape(g, 128, n, -1)
    if fmt == "e4m3":
        vals = words.view(ml_dtypes.float8_e4m3fn).astype(np.float64)
    else:
        nib = np.empty((g, 128, n, 4), np.uint8)
        nib[..., 0::2] = words & 0xF
        nib[..., 1::2] = words >> 4
        vals = E2M1[nib]
    vals = vals * np.repeat(np.exp2(scales.astype(np.float64) - 127.0), 8, axis=1)[..., None]
    return vals.transpose(0, 1, 3, 2).reshape(g * 512, n)


K, J, R, T, U, Z, M, O, N, E, G = 512, 512, 512, 1024, 1024, 512, 1024, 256, 256, 128, 512


def setup_inputs():
    n = np.random.standard_normal
    idx = np.random.permutation(T)[:J]
    idx2 = np.stack([np.random.permutation(U)[:J] for _ in range(8)])
    idx3 = np.random.permutation(M)[:J]
    idx4 = np.stack([np.random.permutation(J)[:O] for _ in range(8)])
    idx5 = np.random.permutation(G)[:O]
    idx6 = np.stack([np.random.permutation(G)[:E] for _ in range(8)])
    idx7 = np.stack([np.random.permutation(O)[:E] for _ in range(8)])
    fk = mx_kscale(K)
    fr = mx_kscale(R)
    fz = mx_kscale(Z)
    wp = pack_weight(n((K, R)) * 1 / np.sqrt(K) / fk[:, None] * fr, "e4m3")
    xop = pack_weight(n((Z, M)) / fz[:, None], "e4m3")
    w2p = pack_weight(n((Z, R)) * 1 / np.sqrt(Z) * fz[:, None] * fr, "e2m1")
    wbp = pack_weight(n((R, N)) * 1 / np.sqrt(R) / fr[:, None], "e2m1")
    wop = pack_weight(n((R, N)) * 1 / np.sqrt(R) / fr[:, None], "e4m3")
    return {
        "ta": (np.random.randint(-7, 8, (K, T)).astype(np.float64)).astype(np.float32),
        "tb": (np.random.randint(-7, 8, (K, U)).astype(np.float64)).astype(np.float32),
        "ga": ((np.random.randint(10, 25, (K, 1)) / 64.0) * fk[:, None]).astype(np.float32),
        "gb": ((np.random.randint(4, 13, (K, 1)) / 64.0) * fk[:, None]).astype(np.float32),
        "w_words": wp[0],
        "w_scales": wp[1],
        "xo_words": xop[0],
        "xo_scales": xop[1],
        "w2_words": w2p[0],
        "w2_scales": w2p[1],
        "sa": (np.random.uniform(0.5, 1.6, (R, 1))).astype(np.float32),
        "wb_words": wbp[0],
        "wb_scales": wbp[1],
        "wo_words": wop[0],
        "wo_scales": wop[1],
        "so": (np.random.uniform(0.5, 1.6, (N, 1))).astype(np.float32),
        "sp": (np.random.uniform(0.5, 1.6, (N, 1))).astype(np.float32),
        "offs": striped(idx),
        "offs2": striped8(idx2),
        "offs3": striped(idx3),
        "offs4": striped8(idx4),
        "offs5": striped(idx5),
        "offs6": striped8(idx6),
        "offs7": striped8(idx7),
    }


def reference(ta, tb, ga, gb, w_words, w_scales, xo_words, xo_scales, w2_words, w2_scales, sa, wb_words, wb_scales, wo_words, wo_scales, so, sp, offs, offs2, offs3, offs4, offs5, offs6, offs7):
    idx = unstriped(offs)
    idx2 = unstriped8(offs2)
    idx3 = unstriped(offs3)
    idx4 = unstriped8(offs4)
    idx5 = unstriped(offs5)
    idx6 = unstriped8(offs6)
    idx7 = unstriped8(offs7)
    wu = unpack_weight(w_words, w_scales, "e4m3")
    xou = unpack_weight(xo_words, xo_scales, "e4m3")
    w2u = unpack_weight(w2_words, w2_scales, "e2m1")
    wbu = unpack_weight(wb_words, wb_scales, "e2m1")
    wou = unpack_weight(wo_words, wo_scales, "e4m3")
    xc = f64(ta)[:, idx] * f64(ga) + pick8(f64(tb), idx2, 64) * f64(gb)
    xcq = mxq(xc, 0, "e4m3")
    xoidx3g = xou[:, idx3]
    a = wu.T @ xcq + w2u.T @ xoidx3g
    g1 = np.maximum(a, 0.0)
    hid = pick8(g1, idx4, 64) * f64(sa)
    hidq = mxq(hid, 0, "e4m3")
    p = wbu.T @ hidq
    q = wou.T @ hidq
    m0 = np.zeros((N, G))
    m0[:, idx5] = p
    y = np.maximum(pick8(m0, idx6, 16) * f64(so), pick8(q, idx7, 16) * f64(sp))
    return y

@@ -1,0 +1,239 @@
+from contextlib import ExitStack
+
+import concourse.mybir as mybir
+
+K, J, R, T, Z, M, O, N, E, G = 512, 512, 512, 1024, 512, 1024, 256, 256, 128, 512
+FLOPS = 2 * (K * R * J + Z * R * J + 2 * R * N * O)
+
+F32 = mybir.dt.float32
+BF16 = mybir.dt.bfloat16
+I32 = mybir.dt.int32
+U32 = mybir.dt.uint32
+U16 = mybir.dt.uint16
+U8 = mybir.dt.uint8
+FP8X4 = mybir.dt.float8_e4m3fn_x4
+FP4X4 = mybir.dt.float4_e2m1fn_x4
+COPY = mybir.ActivationFunctionType.Copy
+RELU = mybir.ActivationFunctionType.Relu
+ADD = mybir.AluOpType.add
+MAX = mybir.AluOpType.max
+
+P = 128
+PACK = 4
+QUADS = 4
+HALF = J // 2
+PER_COL = 16
+FP8_PLANE = 4
+
+
+def tile_picked_basedetail_plain_bank_kept_outcomes_outboard_kernel(
+    tc, ta, tb, ga, gb, w_words, w_scales, xo_words, xo_scales, w2_words, w2_scales, sa,
+    wb_words, wb_scales, wo_words, wo_scales, so, sp,
+    offs, offs2, offs3, offs4, offs5, offs6, offs7, out,
+):
+    nc = tc.nc
+    with ExitStack() as ctx:
+        lists = ctx.enter_context(tc.tile_pool(name="lists", bufs=1))
+        sb = ctx.enter_context(tc.tile_pool(name="sb", bufs=1))
+        psum = ctx.enter_context(tc.psum_pool(name="psum", bufs=1))
+
+        def new(name, shape, dtype):
+            return sb.tile(shape, dtype, name=name, align_bytes=64)
+
+        def load_list(name, src):
+            tile = lists.tile(list(src.shape), U16, name=name)
+            nc.sync.dma_start(tile[:], src)
+            return tile
+
+        def load_words(name, src, dtype):
+            flat = src[0] if src.ndim == 3 else src[0].rearrange("p c b -> p (c b)")
+            width = flat.shape[1] // (4 if dtype == U32 else 1)
+            tile = new(name, [P, width], dtype)
+            nc.sync.dma_start(out=tile[:].bitcast(I32), in_=flat.bitcast(I32))
+            return tile
+
+        def load_plane(name, table, t):
+            tile = new(name, [P, T], F32)
+            nc.sync.dma_start(out=tile[:], in_=table.rearrange("(p t) c -> p t c", t=PACK)[:, t, :])
+            return tile
+
+        def load_by_word(queue, name, vec):
+            tile = new(name, [P, PACK], F32)
+            queue.dma_start(out=tile[:], in_=vec.rearrange("(p t) o -> p (t o)", t=PACK))
+            return tile
+
+        def load_by_tile(name, vec):
+            tile = new(name, [P, N // P], F32)
+            with nc.allow_non_contiguous_dma(reason="one float a partition and tile"):
+                nc.sync.dma_start(out=tile[:], in_=vec.rearrange("(c p) o -> p (c o)", p=P))
+            return tile
+
+        def by_quadrant(scales):
+            return scales[0].rearrange("(q r) c -> r q c", r=4).bitcast(I32)
+
+        def deal(src, dst, run):
+            return dict(
+                out=dst.rearrange("p (t c i) -> p c t i", t=PACK, i=run),
+                in_=src.rearrange("p (c i t) -> p c t i", t=PACK, i=run),
+            )
+
+        def interleave(dst, planes):
+            nc.vector.tensor_copy(
+                out=dst.rearrange("p (c i t) -> p c t i", t=PACK, i=4),
+                in_=planes.rearrange("p t (c i) -> p c t i", i=4),
+            )
+
+        xo_stage = new("xo_stage", [4, QUADS, M // 4], I32)
+        w_stage = new("w_stage", [P, QUADS, (R + N) // 4], I32)
+        nc.vector.memset(w_stage[64:96], 0)
+        lo, hi = slice(64, 68), slice(64 + FP8_PLANE, 64 + FP8_PLANE + 4)
+        first, second = slice(0, R // 4), slice(R // 4, (R + N) // 4)
+        xo_plane = new("xo_plane", [P, M], U8)
+        nc.vector.memset(xo_plane[:].bitcast(I32), 0)
+        boards = [new("board%d" % c, [P, G], F32) for c in range(N // P)]
+        for board in boards:
+            nc.vector.memset(board[:], 0.0)
+
+        ta_sb, tb_sb = [], []
+        ta_sb.append(load_plane("ta0", ta, 0))
+        ga_sb = load_by_word(nc.scalar, "ga_sb", ga)
+        nc.scalar.dma_start(out=xo_stage[:], in_=by_quadrant(xo_scales))
+        gb_sb = load_by_word(nc.gpsimd, "gb_sb", gb)
+        base_list = load_list("base_list", offs)
+        tb_sb.append(load_plane("tb0", tb, 0))
+        detail_list = load_list("detail_list", offs2)
+        note_list = load_list("note_list", offs3)
+        ta_sb.append(load_plane("ta1", ta, 1))
+        tb_sb.append(load_plane("tb1", tb, 1))
+        nc.sync.dma_start(out=w_stage[hi, :, first], in_=by_quadrant(w_scales))
+        nc.sync.dma_start(out=w_stage[lo, :, first], in_=by_quadrant(w2_scales))
+        xo_sb = load_words("xo_sb", xo_words, U32)
+        nc.sync.dma_start(out=w_stage[lo, :, second], in_=by_quadrant(wb_scales))
+        ta_sb.append(load_plane("ta2", ta, 2))
+        nc.sync.dma_start(out=w_stage[hi, :, second], in_=by_quadrant(wo_scales))
+        w2_sb = load_words("w2_sb", w2_words, U8)
+        tb_sb.append(load_plane("tb2", tb, 2))
+        ta_sb.append(load_plane("ta3", ta, 3))
+        tb_sb.append(load_plane("tb3", tb, 3))
+        w_sb = load_words("w_sb", w_words, U32)
+        slot_list = load_list("slot_list", offs4)
+        sa_sb = load_by_word(nc.sync, "sa_sb", sa)
+        wb_sb = load_words("wb_sb", wb_words, U8)
+        wo_sb = load_words("wo_sb", wo_words, U32)
+        board_list = load_list("board_list", offs5)
+        first_list = load_list("first_list", offs6)
+        second_list = load_list("second_list", offs7)
+        so_sb = load_by_tile("so_sb", so)
+        sp_sb = load_by_tile("sp_sb", sp)
+
+        w_planes = new("w_planes", [P, R + N], U8)
+        for q in range(QUADS):
+            nc.vector.tensor_copy(out=xo_plane[32 * q : 32 * q + 4, :].bitcast(I32), in_=xo_stage[:, q, :])
+        xo_scale = new("xo_scale", [P, J], U8)
+        nc.vector.tensor_copy(out=xo_scale[:], in_=xo_plane[:].indirect(note_list[:]))
+        for q in range(QUADS):
+            nc.vector.tensor_copy(out=w_planes[32 * q : 32 * q + 32, :].bitcast(I32), in_=w_stage[64:96, q, :])
+        a_scale = new("a_scale", [P, R], U8)
+        nc.vector.tensor_copy(**deal(w_planes[:, 0:R], a_scale[:], 16))
+
+        last = PACK - 1
+        base = [new("base%d" % t, [P, J], F32) for t in range(PACK)]
+        detail = [new("detail%d" % t, [P, J], F32) for t in range(PACK)]
+        xc_planes = new("xc_planes", [P, last, J], BF16)
+        halves = [slice(h * HALF, (h + 1) * HALF) for h in range(2)]
+        half_cols = [slice(h * HALF // PER_COL, (h + 1) * HALF // PER_COL) for h in range(2)]
+        xo_code = new("xo_code", [P, J], U32)
+        w2_code = new("w2_code", [P, 2 * R], U8)
+        xc_bf = [new("xc_bf%d" % h, [P, HALF, PACK], BF16) for h in range(2)]
+        xc_code = [new("xc_code%d" % h, [P, HALF], U32) for h in range(2)]
+        xc_scale = [new("xc_scale%d" % h, [P, HALF], U8) for h in range(2)]
+        for t in range(PACK):
+            nc.scalar.activation(out=base[t][:], in_=ta_sb[t][:].indirect(base_list[:]), func=COPY, scale=ga_sb[:, t : t + 1])
+            if t < last:
+                nc.scalar.activation(out=detail[t][:], in_=tb_sb[t][:].indirect(detail_list[:]), func=COPY, scale=gb_sb[:, t : t + 1])
+                nc.vector.tensor_tensor(out=xc_planes[:, t, :], in0=base[t][:], in1=detail[t][:], op=ADD)
+            if t == 1:
+                nc.vector.tensor_copy(out=xo_code[:], in_=xo_sb[:].indirect(note_list[:]))
+                nc.vector.tensor_copy(**deal(w2_sb[:].bitcast(U16), w2_code[:].bitcast(U16), 8))
+        for h in range(2):
+            nc.vector.tensor_copy(out=xc_bf[h][:, :, 0:last], in_=xc_planes[:, :, halves[h]].rearrange("p t j -> p j t"))
+        for h in range(2):
+            nc.scalar.activation(
+                out=detail[last][:, halves[h]], in_=tb_sb[last][:].indirect(detail_list[:, half_cols[h]]),
+                func=COPY, scale=gb_sb[:, last : last + 1],
+            )
+            nc.vector.tensor_tensor(out=xc_bf[h][:, :, last], in0=base[last][:, halves[h]], in1=detail[last][:, halves[h]], op=ADD)
+        for h in range(2):
+            nc.vector.quantize_mx(
+                out=xc_code[h][:].bitcast(FP8X4), scales=xc_scale[h][:], in_=xc_bf[h][:].rearrange("p j t -> p (j t)")
+            )
+
+        w_code = new("w_code", [P, R], U32)
+        nc.scalar.copy(**deal(w_sb[:], w_code[:], 4))
+
+        kept = [new("kept%d" % t, [P, J], F32) for t in range(PACK)]
+        parts = [(t, h) for t in range(PACK) for h in range(2)]
+        banks = {}
+        for t, h in parts:
+            banks[t, h] = psum.tile([P, HALF], F32, name="bank%d" % (PACK * h + t))
+            nc.tensor.matmul_mx(
+                out=banks[t, h][:], start=True, stop=False,
+                lhsT=w2_code[:, 2 * t * P : 2 * (t + 1) * P].bitcast(FP4X4), lhsT_scale=a_scale[:, t * P : (t + 1) * P],
+                rhs=xo_code[:, halves[h]].bitcast(FP8X4), rhs_scale=xo_scale[:, halves[h]],
+            )
+        for t, h in parts:
+            nc.tensor.matmul_mx(
+                out=banks[t, h][:], start=False, stop=True,
+                lhsT=w_code[:, t * P : (t + 1) * P].bitcast(FP8X4), lhsT_scale=a_scale[FP8_PLANE:, t * P : (t + 1) * P],
+                rhs=xc_code[h][:].bitcast(FP8X4), rhs_scale=xc_scale[h][:],
+            )
+            if h == 0 and t < 2:
+                nc.scalar.activation(out=kept[t][:, halves[h]], in_=banks[t, h][:], func=RELU)
+            else:
+                nc.vector.tensor_scalar_max(out=kept[t][:, halves[h]], in0=banks[t, h][:], scalar1=0.0)
+
+        hid_planes = new("hid_planes", [P, PACK, O], BF16)
+        for t in range(PACK):
+            nc.scalar.activation(out=hid_planes[:, t, :], in_=kept[t][:].indirect(slot_list[:]), func=COPY, scale=sa_sb[:, t : t + 1])
+        hid_bf = new("hid_bf", [P, O, PACK], BF16)
+        hid_code = new("hid_code", [P, O], U32)
+        hid_scale = new("hid_scale", [P, O], U8)
+        nc.vector.tensor_copy(out=hid_bf[:, :, 0:last], in_=hid_planes[:, 0:last, :].rearrange("p t o -> p o t"))
+        nc.vector.tensor_copy(out=hid_bf[:, :, last], in_=hid_planes[:, last, :])
+        nc.vector.quantize_mx(
+            out=hid_code[:].bitcast(FP8X4), scales=hid_scale[:], in_=hid_bf[:].rearrange("p o t -> p (o t)")
+        )
+
+        moving = dict(rhs=hid_code[:].bitcast(FP8X4), rhs_scale=hid_scale[:], start=True, stop=True)
+        p_acc = [psum.tile([P, O], F32, name="bank%d" % c) for c in range(2)]
+        q_acc = [psum.tile([P, O], F32, name="bank%d" % (2 + c)) for c in range(2)]
+        p_sb = [new("p_sb%d" % c, [P, O], F32) for c in range(2)]
+        q_sb = [new("q_sb%d" % c, [P, O], F32) for c in range(2)]
+        for c in range(2):
+            nc.tensor.matmul_mx(
+                out=p_acc[c][:], lhsT=wb_sb[:, 2 * c * P : 2 * (c + 1) * P].bitcast(FP4X4),
+                lhsT_scale=w_planes[:, R + c * P : R + (c + 1) * P], **moving,
+            )
+        for c in range(2):
+            nc.tensor.matmul_mx(
+                out=q_acc[c][:], lhsT=wo_sb[:, c * P : (c + 1) * P].bitcast(FP8X4),
+                lhsT_scale=w_planes[FP8_PLANE:, R + c * P : R + (c + 1) * P], **moving,
+            )
+        mid, mid_col = O // 2, O // 2 // PER_COL
+        nc.vector.tensor_copy(out=p_sb[0][:], in_=p_acc[0][:])
+        nc.scalar.copy(out=p_sb[1][:], in_=p_acc[1][:])
+        nc.vector.tensor_copy(out=boards[0][:].indirect(board_list[:]), in_=p_sb[0][:])
+        nc.scalar.activation(out=boards[1][:].indirect(board_list[:, :mid_col]), in_=p_sb[1][:, :mid], func=COPY)
+        nc.vector.tensor_copy(out=boards[1][:].indirect(board_list[:, mid_col:]), in_=p_sb[1][:, mid:])
+        for c in range(2):
+            nc.scalar.copy(out=q_sb[c][:], in_=q_acc[c][:])
+
+        left = [new("left%d" % c, [P, E], F32) for c in range(2)]
+        right = [new("right%d" % c, [P, E], F32) for c in range(2)]
+        best = [new("best%d" % c, [P, E], F32) for c in range(2)]
+        for c in range(2):
+            nc.scalar.activation(out=right[c][:], in_=q_sb[c][:].indirect(second_list[:]), func=COPY, scale=sp_sb[:, c : c + 1])
+        for c in range(2):
+            nc.scalar.activation(out=left[c][:], in_=boards[c][:].indirect(first_list[:]), func=COPY, scale=so_sb[:, c : c + 1])
+            nc.vector.tensor_tensor(out=best[c][:], in0=left[c][:], in1=right[c][:], op=MAX)
+            nc.sync.dma_start(out=out[c * P : (c + 1) * P, :], in_=best[c][:])

@@ -84,49 +84,55 @@ def tile_picked_basedetail_plain_bank_kept_outcomes_outboard_kernel(
             )
 
         xo_stage = new("xo_stage", [4, QUADS, M // 4], I32)
-        w_stage = new("w_stage", [P, QUADS, (R + N) // 4], I32)
+        nc.gpsimd.dma_start(out=xo_stage[:], in_=by_quadrant(xo_scales))
+        w_stage = new("w_stage", [P, QUADS, R // 4], I32)
         nc.vector.memset(w_stage[64:96], 0)
-        lo, hi = slice(64, 68), slice(64 + FP8_PLANE, 64 + FP8_PLANE + 4)
-        first, second = slice(0, R // 4), slice(R // 4, (R + N) // 4)
+        nc.gpsimd.dma_start(out=w_stage[64:68], in_=by_quadrant(w2_scales))
         xo_plane = new("xo_plane", [P, M], U8)
         nc.vector.memset(xo_plane[:].bitcast(I32), 0)
+        out_planes = new("out_planes", [P, 2 * N], U8)
+        nc.vector.memset(out_planes[:].bitcast(I32), 0)
         boards = [new("board%d" % c, [P, G], F32) for c in range(N // P)]
         for board in boards:
             nc.vector.memset(board[:], 0.0)
 
+        def load_scale_rows(cols, scales):
+            for q in range(QUADS):
+                nc.sync.dma_start(
+                    out=out_planes[32 * q : 32 * q + 4, cols].bitcast(I32), in_=scales[0][4 * q : 4 * q + 4, :].bitcast(I32)
+                )
+
         ta_sb, tb_sb = [], []
         ta_sb.append(load_plane("ta0", ta, 0))
         ga_sb = load_by_word(nc.scalar, "ga_sb", ga)
-        nc.scalar.dma_start(out=xo_stage[:], in_=by_quadrant(xo_scales))
-        gb_sb = load_by_word(nc.gpsimd, "gb_sb", gb)
+        gb_sb = load_by_word(nc.scalar, "gb_sb", gb)
         base_list = load_list("base_list", offs)
         tb_sb.append(load_plane("tb0", tb, 0))
         detail_list = load_list("detail_list", offs2)
         note_list = load_list("note_list", offs3)
         ta_sb.append(load_plane("ta1", ta, 1))
         tb_sb.append(load_plane("tb1", tb, 1))
-        nc.sync.dma_start(out=w_stage[hi, :, first], in_=by_quadrant(w_scales))
-        nc.sync.dma_start(out=w_stage[lo, :, first], in_=by_quadrant(w2_scales))
+        nc.sync.dma_start(out=w_stage[64 + FP8_PLANE : 68 + FP8_PLANE], in_=by_quadrant(w_scales))
         xo_sb = load_words("xo_sb", xo_words, U32)
-        nc.sync.dma_start(out=w_stage[lo, :, second], in_=by_quadrant(wb_scales))
         ta_sb.append(load_plane("ta2", ta, 2))
-        nc.sync.dma_start(out=w_stage[hi, :, second], in_=by_quadrant(wo_scales))
-        w2_sb = load_words("w2_sb", w2_words, U8)
         tb_sb.append(load_plane("tb2", tb, 2))
         ta_sb.append(load_plane("ta3", ta, 3))
+        w2_sb = load_words("w2_sb", w2_words, U8)
         tb_sb.append(load_plane("tb3", tb, 3))
         w_sb = load_words("w_sb", w_words, U32)
         slot_list = load_list("slot_list", offs4)
         sa_sb = load_by_word(nc.sync, "sa_sb", sa)
         wb_sb = load_words("wb_sb", wb_words, U8)
+        load_scale_rows(slice(0, N), wb_scales)
         wo_sb = load_words("wo_sb", wo_words, U32)
+        load_scale_rows(slice(N, 2 * N), wo_scales)
         board_list = load_list("board_list", offs5)
-        first_list = load_list("first_list", offs6)
         second_list = load_list("second_list", offs7)
-        so_sb = load_by_tile("so_sb", so)
         sp_sb = load_by_tile("sp_sb", sp)
+        first_list = load_list("first_list", offs6)
+        so_sb = load_by_tile("so_sb", so)
 
-        w_planes = new("w_planes", [P, R + N], U8)
+        w_planes = new("w_planes", [P, R], U8)
         for q in range(QUADS):
             nc.vector.tensor_copy(out=xo_plane[32 * q : 32 * q + 4, :].bitcast(I32), in_=xo_stage[:, q, :])
         xo_scale = new("xo_scale", [P, J], U8)
@@ -134,35 +140,41 @@ def tile_picked_basedetail_plain_bank_kept_outcomes_outboard_kernel(
         for q in range(QUADS):
             nc.vector.tensor_copy(out=w_planes[32 * q : 32 * q + 32, :].bitcast(I32), in_=w_stage[64:96, q, :])
         a_scale = new("a_scale", [P, R], U8)
-        nc.vector.tensor_copy(**deal(w_planes[:, 0:R], a_scale[:], 16))
+        nc.vector.tensor_copy(**deal(w_planes[:], a_scale[:], 16))
 
-        last = PACK - 1
-        base = [new("base%d" % t, [P, J], F32) for t in range(PACK)]
-        detail = [new("detail%d" % t, [P, J], F32) for t in range(PACK)]
-        xc_planes = new("xc_planes", [P, last, J], BF16)
         halves = [slice(h * HALF, (h + 1) * HALF) for h in range(2)]
         half_cols = [slice(h * HALF // PER_COL, (h + 1) * HALF // PER_COL) for h in range(2)]
+        base = [new("base%d" % u, [P, 2, J], F32) for u in range(2)]
+        early = new("early", [P, 2, J], F32)
+        late = [new("late%d" % h, [P, 2, HALF], F32) for h in range(2)]
         xo_code = new("xo_code", [P, J], U32)
         w2_code = new("w2_code", [P, 2 * R], U8)
         xc_bf = [new("xc_bf%d" % h, [P, HALF, PACK], BF16) for h in range(2)]
         xc_code = [new("xc_code%d" % h, [P, HALF], U32) for h in range(2)]
         xc_scale = [new("xc_scale%d" % h, [P, HALF], U8) for h in range(2)]
-        for t in range(PACK):
-            nc.scalar.activation(out=base[t][:], in_=ta_sb[t][:].indirect(base_list[:]), func=COPY, scale=ga_sb[:, t : t + 1])
-            if t < last:
-                nc.scalar.activation(out=detail[t][:], in_=tb_sb[t][:].indirect(detail_list[:]), func=COPY, scale=gb_sb[:, t : t + 1])
-                nc.vector.tensor_tensor(out=xc_planes[:, t, :], in0=base[t][:], in1=detail[t][:], op=ADD)
-            if t == 1:
-                nc.vector.tensor_copy(out=xo_code[:], in_=xo_sb[:].indirect(note_list[:]))
-                nc.vector.tensor_copy(**deal(w2_sb[:].bitcast(U16), w2_code[:].bitcast(U16), 8))
-        for h in range(2):
-            nc.vector.tensor_copy(out=xc_bf[h][:, :, 0:last], in_=xc_planes[:, :, halves[h]].rearrange("p t j -> p j t"))
-        for h in range(2):
-            nc.scalar.activation(
-                out=detail[last][:, halves[h]], in_=tb_sb[last][:].indirect(detail_list[:, half_cols[h]]),
-                func=COPY, scale=gb_sb[:, last : last + 1],
+
+        def fetch(dst, window, offsets, scale):
+            nc.scalar.activation(out=dst, in_=window[:].indirect(offsets), func=COPY, scale=scale)
+
+        def add_pair(h, u, detail):
+            nc.vector.tensor_tensor(
+                out=xc_bf[h][:, :, 2 * u : 2 * u + 2],
+                in0=base[u][:, :, halves[h]].rearrange("p t j -> p j t"), in1=detail.rearrange("p t j -> p j t"), op=ADD,
             )
-            nc.vector.tensor_tensor(out=xc_bf[h][:, :, last], in0=base[last][:, halves[h]], in1=detail[last][:, halves[h]], op=ADD)
+
+        for t in (0, 1):
+            fetch(base[0][:, t, :], ta_sb[t], base_list[:], ga_sb[:, t : t + 1])
+            fetch(early[:, t, :], tb_sb[t], detail_list[:], gb_sb[:, t : t + 1])
+        for h in range(2):
+            add_pair(h, 0, early[:, :, halves[h]])
+        nc.vector.tensor_copy(out=xo_code[:], in_=xo_sb[:].indirect(note_list[:]))
+        nc.vector.tensor_copy(**deal(w2_sb[:].bitcast(U16), w2_code[:].bitcast(U16), 8))
+        for t in (2, 3):
+            fetch(base[1][:, t - 2, :], ta_sb[t], base_list[:], ga_sb[:, t : t + 1])
+            for h in range(2):
+                fetch(late[h][:, t - 2, :], tb_sb[t], detail_list[:, half_cols[h]], gb_sb[:, t : t + 1])
+        for h in range(2):
+            add_pair(h, 1, late[h][:])
         for h in range(2):
             nc.vector.quantize_mx(
                 out=xc_code[h][:].bitcast(FP8X4), scales=xc_scale[h][:], in_=xc_bf[h][:].rearrange("p j t -> p (j t)")
@@ -192,14 +204,14 @@ def tile_picked_basedetail_plain_bank_kept_outcomes_outboard_kernel(
             else:
                 nc.vector.tensor_scalar_max(out=kept[t][:, halves[h]], in0=banks[t, h][:], scalar1=0.0)
 
-        hid_planes = new("hid_planes", [P, PACK, O], BF16)
-        for t in range(PACK):
-            nc.scalar.activation(out=hid_planes[:, t, :], in_=kept[t][:].indirect(slot_list[:]), func=COPY, scale=sa_sb[:, t : t + 1])
+        hid_pairs = [new("hid_pair%d" % u, [P, 2, O], BF16) for u in range(2)]
         hid_bf = new("hid_bf", [P, O, PACK], BF16)
         hid_code = new("hid_code", [P, O], U32)
         hid_scale = new("hid_scale", [P, O], U8)
-        nc.vector.tensor_copy(out=hid_bf[:, :, 0:last], in_=hid_planes[:, 0:last, :].rearrange("p t o -> p o t"))
-        nc.vector.tensor_copy(out=hid_bf[:, :, last], in_=hid_planes[:, last, :])
+        for u in range(2):
+            for t in (2 * u, 2 * u + 1):
+                fetch(hid_pairs[u][:, t % 2, :], kept[t], slot_list[:], sa_sb[:, t : t + 1])
+            nc.vector.tensor_copy(out=hid_bf[:, :, 2 * u : 2 * u + 2], in_=hid_pairs[u][:].rearrange("p t o -> p o t"))
         nc.vector.quantize_mx(
             out=hid_code[:].bitcast(FP8X4), scales=hid_scale[:], in_=hid_bf[:].rearrange("p o t -> p (o t)")
         )
@@ -212,12 +224,12 @@ def tile_picked_basedetail_plain_bank_kept_outcomes_outboard_kernel(
         for c in range(2):
             nc.tensor.matmul_mx(
                 out=p_acc[c][:], lhsT=wb_sb[:, 2 * c * P : 2 * (c + 1) * P].bitcast(FP4X4),
-                lhsT_scale=w_planes[:, R + c * P : R + (c + 1) * P], **moving,
+                lhsT_scale=out_planes[:, c * P : (c + 1) * P], **moving,
             )
         for c in range(2):
             nc.tensor.matmul_mx(
                 out=q_acc[c][:], lhsT=wo_sb[:, c * P : (c + 1) * P].bitcast(FP8X4),
-                lhsT_scale=w_planes[FP8_PLANE:, R + c * P : R + (c + 1) * P], **moving,
+                lhsT_scale=out_planes[:, N + c * P : N + (c + 1) * P], **moving,
             )
         mid, mid_col = O // 2, O // 2 // PER_COL
         nc.vector.tensor_copy(out=p_sb[0][:], in_=p_acc[0][:])

@@ -103,22 +103,22 @@ def tile_picked_basedetail_plain_bank_kept_outcomes_outboard_kernel(
                 )
 
         ta_sb, tb_sb = [], []
-        ta_sb.append(load_plane("ta0", ta, 0))
-        ga_sb = load_by_word(nc.scalar, "ga_sb", ga)
-        gb_sb = load_by_word(nc.scalar, "gb_sb", gb)
-        base_list = load_list("base_list", offs)
         tb_sb.append(load_plane("tb0", tb, 0))
+        gb_sb = load_by_word(nc.scalar, "gb_sb", gb)
+        ga_sb = load_by_word(nc.scalar, "ga_sb", ga)
         detail_list = load_list("detail_list", offs2)
+        ta_sb.append(load_plane("ta0", ta, 0))
+        base_list = load_list("base_list", offs)
         note_list = load_list("note_list", offs3)
-        ta_sb.append(load_plane("ta1", ta, 1))
         tb_sb.append(load_plane("tb1", tb, 1))
         nc.sync.dma_start(out=w_stage[64 + FP8_PLANE : 68 + FP8_PLANE], in_=by_quadrant(w_scales))
         xo_sb = load_words("xo_sb", xo_words, U32)
-        ta_sb.append(load_plane("ta2", ta, 2))
+        ta_sb.append(load_plane("ta1", ta, 1))
         tb_sb.append(load_plane("tb2", tb, 2))
-        ta_sb.append(load_plane("ta3", ta, 3))
-        w2_sb = load_words("w2_sb", w2_words, U8)
+        ta_sb.append(load_plane("ta2", ta, 2))
         tb_sb.append(load_plane("tb3", tb, 3))
+        w2_sb = load_words("w2_sb", w2_words, U8)
+        ta_sb.append(load_plane("ta3", ta, 3))
         w_sb = load_words("w_sb", w_words, U32)
         slot_list = load_list("slot_list", offs4)
         sa_sb = load_by_word(nc.sync, "sa_sb", sa)
@@ -143,10 +143,10 @@ def tile_picked_basedetail_plain_bank_kept_outcomes_outboard_kernel(
         nc.vector.tensor_copy(**deal(w_planes[:], a_scale[:], 16))
 
         halves = [slice(h * HALF, (h + 1) * HALF) for h in range(2)]
-        half_cols = [slice(h * HALF // PER_COL, (h + 1) * HALF // PER_COL) for h in range(2)]
-        base = [new("base%d" % u, [P, 2, J], F32) for u in range(2)]
+        detail = [new("detail%d" % u, [P, 2, J], F32) for u in range(2)]
         early = new("early", [P, 2, J], F32)
-        late = [new("late%d" % h, [P, 2, HALF], F32) for h in range(2)]
+        pieces = [(0, HALF // 2), (HALF // 2, HALF), (HALF, J)]
+        late = [new("late%d" % lo, [P, 2, hi - lo], F32) for lo, hi in pieces]
         xo_code = new("xo_code", [P, J], U32)
         w2_code = new("w2_code", [P, 2 * R], U8)
         xc_bf = [new("xc_bf%d" % h, [P, HALF, PACK], BF16) for h in range(2)]
@@ -156,25 +156,26 @@ def tile_picked_basedetail_plain_bank_kept_outcomes_outboard_kernel(
         def fetch(dst, window, offsets, scale):
             nc.scalar.activation(out=dst, in_=window[:].indirect(offsets), func=COPY, scale=scale)
 
-        def add_pair(h, u, detail):
+        def add_pair(u, lo, hi, base):
+            h = lo // HALF
             nc.vector.tensor_tensor(
-                out=xc_bf[h][:, :, 2 * u : 2 * u + 2],
-                in0=base[u][:, :, halves[h]].rearrange("p t j -> p j t"), in1=detail.rearrange("p t j -> p j t"), op=ADD,
+                out=xc_bf[h][:, lo - h * HALF : hi - h * HALF, 2 * u : 2 * u + 2],
+                in0=base.rearrange("p t j -> p j t"), in1=detail[u][:, :, lo:hi].rearrange("p t j -> p j t"), op=ADD,
             )
 
-        for t in (0, 1):
-            fetch(base[0][:, t, :], ta_sb[t], base_list[:], ga_sb[:, t : t + 1])
-            fetch(early[:, t, :], tb_sb[t], detail_list[:], gb_sb[:, t : t + 1])
-        for h in range(2):
-            add_pair(h, 0, early[:, :, halves[h]])
         nc.vector.tensor_copy(out=xo_code[:], in_=xo_sb[:].indirect(note_list[:]))
+        for t in (0, 1):
+            fetch(detail[0][:, t, :], tb_sb[t], detail_list[:], gb_sb[:, t : t + 1])
+            fetch(early[:, t, :], ta_sb[t], base_list[:], ga_sb[:, t : t + 1])
+        for h in range(2):
+            add_pair(0, h * HALF, (h + 1) * HALF, early[:, :, halves[h]])
         nc.vector.tensor_copy(**deal(w2_sb[:].bitcast(U16), w2_code[:].bitcast(U16), 8))
         for t in (2, 3):
-            fetch(base[1][:, t - 2, :], ta_sb[t], base_list[:], ga_sb[:, t : t + 1])
-            for h in range(2):
-                fetch(late[h][:, t - 2, :], tb_sb[t], detail_list[:, half_cols[h]], gb_sb[:, t : t + 1])
-        for h in range(2):
-            add_pair(h, 1, late[h][:])
+            fetch(detail[1][:, t - 2, :], tb_sb[t], detail_list[:], gb_sb[:, t : t + 1])
+            for piece, (lo, hi) in zip(late, pieces):
+                fetch(piece[:, t - 2, :], ta_sb[t], base_list[:, lo // PER_COL : hi // PER_COL], ga_sb[:, t : t + 1])
+        for piece, (lo, hi) in zip(late, pieces):
+            add_pair(1, lo, hi, piece[:])
         for h in range(2):
             nc.vector.quantize_mx(
                 out=xc_code[h][:].bitcast(FP8X4), scales=xc_scale[h][:], in_=xc_bf[h][:].rearrange("p j t -> p (j t)")
@@ -204,39 +205,52 @@ def tile_picked_basedetail_plain_bank_kept_outcomes_outboard_kernel(
             else:
                 nc.vector.tensor_scalar_max(out=kept[t][:, halves[h]], in0=banks[t, h][:], scalar1=0.0)
 
-        hid_pairs = [new("hid_pair%d" % u, [P, 2, O], BF16) for u in range(2)]
-        hid_bf = new("hid_bf", [P, O, PACK], BF16)
+        mid = O // 2
+        spans = [slice(h * mid, (h + 1) * mid) for h in range(2)]
+        span_cols = [slice(h * mid // PER_COL, (h + 1) * mid // PER_COL) for h in range(2)]
+        hid_early = new("hid_early", [P, 2, O], BF16)
+        hid_late = [new("hid_late%d" % h, [P, 2, mid], BF16) for h in range(2)]
+        hid_bf = [new("hid_bf%d" % h, [P, mid, PACK], BF16) for h in range(2)]
         hid_code = new("hid_code", [P, O], U32)
         hid_scale = new("hid_scale", [P, O], U8)
-        for u in range(2):
-            for t in (2 * u, 2 * u + 1):
-                fetch(hid_pairs[u][:, t % 2, :], kept[t], slot_list[:], sa_sb[:, t : t + 1])
-            nc.vector.tensor_copy(out=hid_bf[:, :, 2 * u : 2 * u + 2], in_=hid_pairs[u][:].rearrange("p t o -> p o t"))
-        nc.vector.quantize_mx(
-            out=hid_code[:].bitcast(FP8X4), scales=hid_scale[:], in_=hid_bf[:].rearrange("p o t -> p (o t)")
-        )
-
-        moving = dict(rhs=hid_code[:].bitcast(FP8X4), rhs_scale=hid_scale[:], start=True, stop=True)
-        p_acc = [psum.tile([P, O], F32, name="bank%d" % c) for c in range(2)]
-        q_acc = [psum.tile([P, O], F32, name="bank%d" % (2 + c)) for c in range(2)]
-        p_sb = [new("p_sb%d" % c, [P, O], F32) for c in range(2)]
-        q_sb = [new("q_sb%d" % c, [P, O], F32) for c in range(2)]
-        for c in range(2):
-            nc.tensor.matmul_mx(
-                out=p_acc[c][:], lhsT=wb_sb[:, 2 * c * P : 2 * (c + 1) * P].bitcast(FP4X4),
-                lhsT_scale=out_planes[:, c * P : (c + 1) * P], **moving,
+        for t in (0, 1):
+            fetch(hid_early[:, t, :], kept[t], slot_list[:], sa_sb[:, t : t + 1])
+        for h in range(2):
+            nc.vector.tensor_copy(out=hid_bf[h][:, :, 0:2], in_=hid_early[:, :, spans[h]].rearrange("p t o -> p o t"))
+        for t in (2, 3):
+            for h in range(2):
+                fetch(hid_late[h][:, t - 2, :], kept[t], slot_list[:, span_cols[h]], sa_sb[:, t : t + 1])
+        for h in range(2):
+            nc.vector.tensor_copy(out=hid_bf[h][:, :, 2:4], in_=hid_late[h][:].rearrange("p t o -> p o t"))
+        for h in range(2):
+            nc.vector.quantize_mx(
+                out=hid_code[:, spans[h]].bitcast(FP8X4), scales=hid_scale[:, spans[h]],
+                in_=hid_bf[h][:].rearrange("p o t -> p (o t)"),
             )
+
+        p_acc = {(c, h): psum.tile([P, mid], F32, name="bank%d" % (2 * h + c)) for h in range(2) for c in range(2)}
+        q_acc = [psum.tile([P, O], F32, name="bank%d" % (4 + c)) for c in range(2)]
+        p_sb = {(c, h): new("p_sb%d%d" % (c, h), [P, mid], F32) for h in range(2) for c in range(2)}
+        q_sb = [new("q_sb%d" % c, [P, O], F32) for c in range(2)]
+        for h in range(2):
+            for c in range(2):
+                nc.tensor.matmul_mx(
+                    out=p_acc[c, h][:], lhsT=wb_sb[:, 2 * c * P : 2 * (c + 1) * P].bitcast(FP4X4),
+                    lhsT_scale=out_planes[:, c * P : (c + 1) * P],
+                    rhs=hid_code[:, spans[h]].bitcast(FP8X4), rhs_scale=hid_scale[:, spans[h]], start=True, stop=True,
+                )
         for c in range(2):
             nc.tensor.matmul_mx(
                 out=q_acc[c][:], lhsT=wo_sb[:, c * P : (c + 1) * P].bitcast(FP8X4),
-                lhsT_scale=out_planes[:, N + c * P : N + (c + 1) * P], **moving,
+                lhsT_scale=out_planes[:, N + c * P : N + (c + 1) * P],
+                rhs=hid_code[:].bitcast(FP8X4), rhs_scale=hid_scale[:], start=True, stop=True,
             )
-        mid, mid_col = O // 2, O // 2 // PER_COL
-        nc.vector.tensor_copy(out=p_sb[0][:], in_=p_acc[0][:])
-        nc.scalar.copy(out=p_sb[1][:], in_=p_acc[1][:])
-        nc.vector.tensor_copy(out=boards[0][:].indirect(board_list[:]), in_=p_sb[0][:])
-        nc.scalar.activation(out=boards[1][:].indirect(board_list[:, :mid_col]), in_=p_sb[1][:, :mid], func=COPY)
-        nc.vector.tensor_copy(out=boards[1][:].indirect(board_list[:, mid_col:]), in_=p_sb[1][:, mid:])
+        nc.scalar.copy(out=p_sb[0, 0][:], in_=p_acc[0, 0][:])
+        nc.scalar.activation(out=boards[0][:].indirect(board_list[:, span_cols[0]]), in_=p_sb[0, 0][:], func=COPY)
+        for c, h in ((1, 0), (1, 1), (0, 1)):
+            nc.vector.tensor_copy(out=p_sb[c, h][:], in_=p_acc[c, h][:])
+        for c, h in ((1, 0), (1, 1), (0, 1)):
+            nc.vector.tensor_copy(out=boards[c][:].indirect(board_list[:, span_cols[h]]), in_=p_sb[c, h][:])
         for c in range(2):
             nc.scalar.copy(out=q_sb[c][:], in_=q_acc[c][:])
 
@@ -245,7 +259,7 @@ def tile_picked_basedetail_plain_bank_kept_outcomes_outboard_kernel(
         best = [new("best%d" % c, [P, E], F32) for c in range(2)]
         for c in range(2):
             nc.scalar.activation(out=right[c][:], in_=q_sb[c][:].indirect(second_list[:]), func=COPY, scale=sp_sb[:, c : c + 1])
-        for c in range(2):
+        for c in (1, 0):
             nc.scalar.activation(out=left[c][:], in_=boards[c][:].indirect(first_list[:]), func=COPY, scale=so_sb[:, c : c + 1])
             nc.vector.tensor_tensor(out=best[c][:], in0=left[c][:], in1=right[c][:], op=MAX)
             nc.sync.dma_start(out=out[c * P : (c + 1) * P, :], in_=best[c][:])

@@ -20,10 +20,17 @@ MAX = mybir.AluOpType.max
 
 P = 128
 PACK = 4
-QUADS = 4
-HALF = J // 2
+QUAD = 32
+QUADS = P // QUAD
+ROWS = 4
 PER_COL = 16
-FP8_PLANE = 4
+LINE = 16
+WORD = 4
+W_SCALE_AT = 4
+W_STAGE_AT = 64
+SLOT_HALF = J // 2
+PLACE_HALF = O // 2
+OUT_TILES = N // P
 
 
 def tile_picked_basedetail_plain_bank_kept_outcomes_outboard_kernel(
@@ -45,11 +52,14 @@ def tile_picked_basedetail_plain_bank_kept_outcomes_outboard_kernel(
             nc.sync.dma_start(tile[:], src)
             return tile
 
-        def load_words(name, src, dtype):
-            flat = src[0] if src.ndim == 3 else src[0].rearrange("p c b -> p (c b)")
-            width = flat.shape[1] // (4 if dtype == U32 else 1)
-            tile = new(name, [P, width], dtype)
-            nc.sync.dma_start(out=tile[:].bitcast(I32), in_=flat.bitcast(I32))
+        def load_fp8_words(name, src):
+            tile = new(name, [P, src.shape[2]], U32)
+            nc.sync.dma_start(out=tile[:].bitcast(I32), in_=src[0].rearrange("p c b -> p (c b)").bitcast(I32))
+            return tile
+
+        def load_fp4_words(name, src):
+            tile = new(name, [P, src.shape[2]], U8)
+            nc.sync.dma_start(out=tile[:].bitcast(I32), in_=src[0].bitcast(I32))
             return tile
 
         def load_plane(name, table, t):
@@ -57,74 +67,77 @@ def tile_picked_basedetail_plain_bank_kept_outcomes_outboard_kernel(
             nc.sync.dma_start(out=tile[:], in_=table.rearrange("(p t) c -> p t c", t=PACK)[:, t, :])
             return tile
 
-        def load_by_word(queue, name, vec):
+        def load_by_plane(queue, name, vec):
             tile = new(name, [P, PACK], F32)
             queue.dma_start(out=tile[:], in_=vec.rearrange("(p t) o -> p (t o)", t=PACK))
             return tile
 
         def load_by_tile(name, vec):
-            tile = new(name, [P, N // P], F32)
+            tile = new(name, [P, OUT_TILES], F32)
             with nc.allow_non_contiguous_dma(reason="one float a partition and tile"):
                 nc.sync.dma_start(out=tile[:], in_=vec.rearrange("(c p) o -> p (c o)", p=P))
             return tile
 
         def by_quadrant(scales):
-            return scales[0].rearrange("(q r) c -> r q c", r=4).bitcast(I32)
+            return scales[0].rearrange("(q r) c -> r q c", r=ROWS).bitcast(I32)
 
-        def deal(src, dst, run):
+        def deal(src, dst, element_bytes):
+            run = LINE // element_bytes
             return dict(
                 out=dst.rearrange("p (t c i) -> p c t i", t=PACK, i=run),
                 in_=src.rearrange("p (c i t) -> p c t i", t=PACK, i=run),
             )
 
-        def interleave(dst, planes):
-            nc.vector.tensor_copy(
-                out=dst.rearrange("p (c i t) -> p c t i", t=PACK, i=4),
-                in_=planes.rearrange("p t (c i) -> p c t i", i=4),
-            )
+        def entries(offsets, lo, hi):
+            return offsets[:, lo // PER_COL : hi // PER_COL]
 
-        xo_stage = new("xo_stage", [4, QUADS, M // 4], I32)
+        def fetch(dst, window, offsets, scale):
+            nc.scalar.activation(out=dst, in_=window[:].indirect(offsets), func=COPY, scale=scale)
+
+        xo_stage = new("xo_stage", [ROWS, QUADS, M // WORD], I32)
         nc.gpsimd.dma_start(out=xo_stage[:], in_=by_quadrant(xo_scales))
-        w_stage = new("w_stage", [P, QUADS, R // 4], I32)
-        nc.vector.memset(w_stage[64:96], 0)
-        nc.gpsimd.dma_start(out=w_stage[64:68], in_=by_quadrant(w2_scales))
-        xo_plane = new("xo_plane", [P, M], U8)
-        nc.vector.memset(xo_plane[:].bitcast(I32), 0)
-        out_planes = new("out_planes", [P, 2 * N], U8)
-        nc.vector.memset(out_planes[:].bitcast(I32), 0)
-        boards = [new("board%d" % c, [P, G], F32) for c in range(N // P)]
+        w_stage = new("w_stage", [P, QUADS, R // WORD], I32)
+        nc.vector.memset(w_stage[W_STAGE_AT : W_STAGE_AT + QUAD], 0)
+        nc.gpsimd.dma_start(out=w_stage[W_STAGE_AT : W_STAGE_AT + ROWS], in_=by_quadrant(w2_scales))
+        xo_rows = new("xo_rows", [P, M], U8)
+        nc.vector.memset(xo_rows[:].bitcast(I32), 0)
+        out_scale = new("out_scale", [P, 2 * N], U8)
+        nc.vector.memset(out_scale[:].bitcast(I32), 0)
+        boards = [new("board%d" % c, [P, G], F32) for c in range(OUT_TILES)]
         for board in boards:
             nc.vector.memset(board[:], 0.0)
 
         def load_scale_rows(cols, scales):
             for q in range(QUADS):
                 nc.sync.dma_start(
-                    out=out_planes[32 * q : 32 * q + 4, cols].bitcast(I32), in_=scales[0][4 * q : 4 * q + 4, :].bitcast(I32)
+                    out=out_scale[QUAD * q : QUAD * q + ROWS, cols].bitcast(I32),
+                    in_=scales[0][ROWS * q : ROWS * (q + 1), :].bitcast(I32),
                 )
 
         ta_sb, tb_sb = [], []
         tb_sb.append(load_plane("tb0", tb, 0))
-        gb_sb = load_by_word(nc.scalar, "gb_sb", gb)
-        ga_sb = load_by_word(nc.scalar, "ga_sb", ga)
+        gb_sb = load_by_plane(nc.scalar, "gb_sb", gb)
+        ga_sb = load_by_plane(nc.scalar, "ga_sb", ga)
         detail_list = load_list("detail_list", offs2)
         ta_sb.append(load_plane("ta0", ta, 0))
         base_list = load_list("base_list", offs)
         note_list = load_list("note_list", offs3)
         tb_sb.append(load_plane("tb1", tb, 1))
-        nc.sync.dma_start(out=w_stage[64 + FP8_PLANE : 68 + FP8_PLANE], in_=by_quadrant(w_scales))
-        xo_sb = load_words("xo_sb", xo_words, U32)
+        w_rows_at = W_STAGE_AT + W_SCALE_AT
+        nc.sync.dma_start(out=w_stage[w_rows_at : w_rows_at + ROWS], in_=by_quadrant(w_scales))
+        xo_sb = load_fp8_words("xo_sb", xo_words)
         ta_sb.append(load_plane("ta1", ta, 1))
         tb_sb.append(load_plane("tb2", tb, 2))
         ta_sb.append(load_plane("ta2", ta, 2))
         tb_sb.append(load_plane("tb3", tb, 3))
-        w2_sb = load_words("w2_sb", w2_words, U8)
+        w2_sb = load_fp4_words("w2_sb", w2_words)
         ta_sb.append(load_plane("ta3", ta, 3))
-        w_sb = load_words("w_sb", w_words, U32)
+        w_sb = load_fp8_words("w_sb", w_words)
         slot_list = load_list("slot_list", offs4)
-        sa_sb = load_by_word(nc.sync, "sa_sb", sa)
-        wb_sb = load_words("wb_sb", wb_words, U8)
+        sa_sb = load_by_plane(nc.sync, "sa_sb", sa)
+        wb_sb = load_fp4_words("wb_sb", wb_words)
         load_scale_rows(slice(0, N), wb_scales)
-        wo_sb = load_words("wo_sb", wo_words, U32)
+        wo_sb = load_fp8_words("wo_sb", wo_words)
         load_scale_rows(slice(N, 2 * N), wo_scales)
         board_list = load_list("board_list", offs5)
         second_list = load_list("second_list", offs7)
@@ -132,134 +145,147 @@ def tile_picked_basedetail_plain_bank_kept_outcomes_outboard_kernel(
         first_list = load_list("first_list", offs6)
         so_sb = load_by_tile("so_sb", so)
 
-        w_planes = new("w_planes", [P, R], U8)
+        w_rows = new("w_rows", [P, R], U8)
         for q in range(QUADS):
-            nc.vector.tensor_copy(out=xo_plane[32 * q : 32 * q + 4, :].bitcast(I32), in_=xo_stage[:, q, :])
+            nc.vector.tensor_copy(out=xo_rows[QUAD * q : QUAD * q + ROWS, :].bitcast(I32), in_=xo_stage[:, q, :])
         xo_scale = new("xo_scale", [P, J], U8)
-        nc.vector.tensor_copy(out=xo_scale[:], in_=xo_plane[:].indirect(note_list[:]))
+        nc.vector.tensor_copy(out=xo_scale[:], in_=xo_rows[:].indirect(note_list[:]))
         for q in range(QUADS):
-            nc.vector.tensor_copy(out=w_planes[32 * q : 32 * q + 32, :].bitcast(I32), in_=w_stage[64:96, q, :])
+            nc.vector.tensor_copy(
+                out=w_rows[QUAD * q : QUAD * (q + 1), :].bitcast(I32), in_=w_stage[W_STAGE_AT : W_STAGE_AT + QUAD, q, :]
+            )
         a_scale = new("a_scale", [P, R], U8)
-        nc.vector.tensor_copy(**deal(w_planes[:], a_scale[:], 16))
+        nc.vector.tensor_copy(**deal(w_rows[:], a_scale[:], 1))
 
-        halves = [slice(h * HALF, (h + 1) * HALF) for h in range(2)]
+        slot_halves = [slice(h * SLOT_HALF, (h + 1) * SLOT_HALF) for h in range(2)]
+        last_pieces = [(0, SLOT_HALF // 2), (SLOT_HALF // 2, SLOT_HALF), (SLOT_HALF, J)]
         detail = [new("detail%d" % u, [P, 2, J], F32) for u in range(2)]
-        early = new("early", [P, 2, J], F32)
-        pieces = [(0, HALF // 2), (HALF // 2, HALF), (HALF, J)]
-        late = [new("late%d" % lo, [P, 2, hi - lo], F32) for lo, hi in pieces]
+        base = [new("base%d" % u, [P, 2, J], F32) for u in range(2)]
         xo_code = new("xo_code", [P, J], U32)
         w2_code = new("w2_code", [P, 2 * R], U8)
-        xc_bf = [new("xc_bf%d" % h, [P, HALF, PACK], BF16) for h in range(2)]
-        xc_code = [new("xc_code%d" % h, [P, HALF], U32) for h in range(2)]
-        xc_scale = [new("xc_scale%d" % h, [P, HALF], U8) for h in range(2)]
+        xc_bf = [new("xc_bf%d" % h, [P, SLOT_HALF, PACK], BF16) for h in range(2)]
+        xc_code = [new("xc_code%d" % h, [P, SLOT_HALF], U32) for h in range(2)]
+        xc_scale = [new("xc_scale%d" % h, [P, SLOT_HALF], U8) for h in range(2)]
 
-        def fetch(dst, window, offsets, scale):
-            nc.scalar.activation(out=dst, in_=window[:].indirect(offsets), func=COPY, scale=scale)
+        def fetch_plane(t, pieces):
+            u, s = divmod(t, 2)
+            fetch(detail[u][:, s, :], tb_sb[t], detail_list[:], gb_sb[:, t : t + 1])
+            for lo, hi in pieces:
+                fetch(base[u][:, s, lo:hi], ta_sb[t], entries(base_list, lo, hi), ga_sb[:, t : t + 1])
 
-        def add_pair(u, lo, hi, base):
-            h = lo // HALF
+        def add_pair(u, lo, hi):
+            h = lo // SLOT_HALF
             nc.vector.tensor_tensor(
-                out=xc_bf[h][:, lo - h * HALF : hi - h * HALF, 2 * u : 2 * u + 2],
-                in0=base.rearrange("p t j -> p j t"), in1=detail[u][:, :, lo:hi].rearrange("p t j -> p j t"), op=ADD,
+                out=xc_bf[h][:, lo - h * SLOT_HALF : hi - h * SLOT_HALF, 2 * u : 2 * u + 2],
+                in0=base[u][:, :, lo:hi].rearrange("p s j -> p j s"),
+                in1=detail[u][:, :, lo:hi].rearrange("p s j -> p j s"),
+                op=ADD,
             )
 
         nc.vector.tensor_copy(out=xo_code[:], in_=xo_sb[:].indirect(note_list[:]))
-        for t in (0, 1):
-            fetch(detail[0][:, t, :], tb_sb[t], detail_list[:], gb_sb[:, t : t + 1])
-            fetch(early[:, t, :], ta_sb[t], base_list[:], ga_sb[:, t : t + 1])
-        for h in range(2):
-            add_pair(0, h * HALF, (h + 1) * HALF, early[:, :, halves[h]])
-        nc.vector.tensor_copy(**deal(w2_sb[:].bitcast(U16), w2_code[:].bitcast(U16), 8))
-        for t in (2, 3):
-            fetch(detail[1][:, t - 2, :], tb_sb[t], detail_list[:], gb_sb[:, t : t + 1])
-            for piece, (lo, hi) in zip(late, pieces):
-                fetch(piece[:, t - 2, :], ta_sb[t], base_list[:, lo // PER_COL : hi // PER_COL], ga_sb[:, t : t + 1])
-        for piece, (lo, hi) in zip(late, pieces):
-            add_pair(1, lo, hi, piece[:])
+        fetch_plane(0, [(0, J)])
+        fetch_plane(1, [(0, J)])
+        for half in slot_halves:
+            add_pair(0, half.start, half.stop)
+        nc.vector.tensor_copy(**deal(w2_sb[:].bitcast(U16), w2_code[:].bitcast(U16), 2))
+        fetch_plane(2, [(0, J)])
+        fetch_plane(3, last_pieces)
+        for lo, hi in last_pieces:
+            add_pair(1, lo, hi)
         for h in range(2):
             nc.vector.quantize_mx(
                 out=xc_code[h][:].bitcast(FP8X4), scales=xc_scale[h][:], in_=xc_bf[h][:].rearrange("p j t -> p (j t)")
             )
 
         w_code = new("w_code", [P, R], U32)
-        nc.scalar.copy(**deal(w_sb[:], w_code[:], 4))
+        nc.scalar.copy(**deal(w_sb[:], w_code[:], WORD))
 
         kept = [new("kept%d" % t, [P, J], F32) for t in range(PACK)]
         parts = [(t, h) for t in range(PACK) for h in range(2)]
-        banks = {}
+        on_scalar = [(0, 0), (1, 0)]
+        a_acc = {}
         for t, h in parts:
-            banks[t, h] = psum.tile([P, HALF], F32, name="bank%d" % (PACK * h + t))
+            a_acc[t, h] = psum.tile([P, SLOT_HALF], F32, name="bank%d" % (PACK * h + t))
             nc.tensor.matmul_mx(
-                out=banks[t, h][:], start=True, stop=False,
+                out=a_acc[t, h][:], start=True, stop=False,
                 lhsT=w2_code[:, 2 * t * P : 2 * (t + 1) * P].bitcast(FP4X4), lhsT_scale=a_scale[:, t * P : (t + 1) * P],
-                rhs=xo_code[:, halves[h]].bitcast(FP8X4), rhs_scale=xo_scale[:, halves[h]],
+                rhs=xo_code[:, slot_halves[h]].bitcast(FP8X4), rhs_scale=xo_scale[:, slot_halves[h]],
             )
         for t, h in parts:
             nc.tensor.matmul_mx(
-                out=banks[t, h][:], start=False, stop=True,
-                lhsT=w_code[:, t * P : (t + 1) * P].bitcast(FP8X4), lhsT_scale=a_scale[FP8_PLANE:, t * P : (t + 1) * P],
+                out=a_acc[t, h][:], start=False, stop=True,
+                lhsT=w_code[:, t * P : (t + 1) * P].bitcast(FP8X4), lhsT_scale=a_scale[W_SCALE_AT:, t * P : (t + 1) * P],
                 rhs=xc_code[h][:].bitcast(FP8X4), rhs_scale=xc_scale[h][:],
             )
-            if h == 0 and t < 2:
-                nc.scalar.activation(out=kept[t][:, halves[h]], in_=banks[t, h][:], func=RELU)
+            if (t, h) in on_scalar:
+                nc.scalar.activation(out=kept[t][:, slot_halves[h]], in_=a_acc[t, h][:], func=RELU)
             else:
-                nc.vector.tensor_scalar_max(out=kept[t][:, halves[h]], in0=banks[t, h][:], scalar1=0.0)
+                nc.vector.tensor_scalar_max(out=kept[t][:, slot_halves[h]], in0=a_acc[t, h][:], scalar1=0.0)
 
-        mid = O // 2
-        spans = [slice(h * mid, (h + 1) * mid) for h in range(2)]
-        span_cols = [slice(h * mid // PER_COL, (h + 1) * mid // PER_COL) for h in range(2)]
-        hid_early = new("hid_early", [P, 2, O], BF16)
-        hid_late = [new("hid_late%d" % h, [P, 2, mid], BF16) for h in range(2)]
-        hid_bf = [new("hid_bf%d" % h, [P, mid, PACK], BF16) for h in range(2)]
+        place_halves = [slice(h * PLACE_HALF, (h + 1) * PLACE_HALF) for h in range(2)]
+        hid_pairs = [new("hid_pair%d" % u, [P, 2, O], BF16) for u in range(2)]
+        hid_bf = [new("hid_bf%d" % h, [P, PLACE_HALF, PACK], BF16) for h in range(2)]
         hid_code = new("hid_code", [P, O], U32)
         hid_scale = new("hid_scale", [P, O], U8)
-        for t in (0, 1):
-            fetch(hid_early[:, t, :], kept[t], slot_list[:], sa_sb[:, t : t + 1])
-        for h in range(2):
-            nc.vector.tensor_copy(out=hid_bf[h][:, :, 0:2], in_=hid_early[:, :, spans[h]].rearrange("p t o -> p o t"))
-        for t in (2, 3):
+
+        def fetch_hidden(t, places):
+            u, s = divmod(t, 2)
+            fetch(hid_pairs[u][:, s, places], kept[t], entries(slot_list, places.start, places.stop), sa_sb[:, t : t + 1])
+
+        def weave_pair(u):
             for h in range(2):
-                fetch(hid_late[h][:, t - 2, :], kept[t], slot_list[:, span_cols[h]], sa_sb[:, t : t + 1])
-        for h in range(2):
-            nc.vector.tensor_copy(out=hid_bf[h][:, :, 2:4], in_=hid_late[h][:].rearrange("p t o -> p o t"))
+                nc.vector.tensor_copy(
+                    out=hid_bf[h][:, :, 2 * u : 2 * u + 2], in_=hid_pairs[u][:, :, place_halves[h]].rearrange("p s o -> p o s")
+                )
+
+        fetch_hidden(0, slice(0, O))
+        fetch_hidden(1, slice(0, O))
+        weave_pair(0)
+        fetch_hidden(2, slice(0, O))
+        for half in place_halves:
+            fetch_hidden(3, half)
+        weave_pair(1)
         for h in range(2):
             nc.vector.quantize_mx(
-                out=hid_code[:, spans[h]].bitcast(FP8X4), scales=hid_scale[:, spans[h]],
+                out=hid_code[:, place_halves[h]].bitcast(FP8X4), scales=hid_scale[:, place_halves[h]],
                 in_=hid_bf[h][:].rearrange("p o t -> p (o t)"),
             )
 
-        p_acc = {(c, h): psum.tile([P, mid], F32, name="bank%d" % (2 * h + c)) for h in range(2) for c in range(2)}
-        q_acc = [psum.tile([P, O], F32, name="bank%d" % (4 + c)) for c in range(2)]
-        p_sb = {(c, h): new("p_sb%d%d" % (c, h), [P, mid], F32) for h in range(2) for c in range(2)}
-        q_sb = [new("q_sb%d" % c, [P, O], F32) for c in range(2)]
-        for h in range(2):
-            for c in range(2):
-                nc.tensor.matmul_mx(
-                    out=p_acc[c, h][:], lhsT=wb_sb[:, 2 * c * P : 2 * (c + 1) * P].bitcast(FP4X4),
-                    lhsT_scale=out_planes[:, c * P : (c + 1) * P],
-                    rhs=hid_code[:, spans[h]].bitcast(FP8X4), rhs_scale=hid_scale[:, spans[h]], start=True, stop=True,
-                )
-        for c in range(2):
+        p_parts = [(c, h) for h in range(2) for c in range(OUT_TILES)]
+        p_acc = {(c, h): psum.tile([P, PLACE_HALF], F32, name="bank%d" % (OUT_TILES * h + c)) for c, h in p_parts}
+        q_acc = [psum.tile([P, O], F32, name="bank%d" % (len(p_parts) + c)) for c in range(OUT_TILES)]
+        p_sb = {(c, h): new("p_sb%d%d" % (c, h), [P, PLACE_HALF], F32) for c, h in p_parts}
+        q_sb = [new("q_sb%d" % c, [P, O], F32) for c in range(OUT_TILES)]
+        for c, h in p_parts:
             nc.tensor.matmul_mx(
-                out=q_acc[c][:], lhsT=wo_sb[:, c * P : (c + 1) * P].bitcast(FP8X4),
-                lhsT_scale=out_planes[:, N + c * P : N + (c + 1) * P],
-                rhs=hid_code[:].bitcast(FP8X4), rhs_scale=hid_scale[:], start=True, stop=True,
+                out=p_acc[c, h][:], start=True, stop=True,
+                lhsT=wb_sb[:, 2 * c * P : 2 * (c + 1) * P].bitcast(FP4X4), lhsT_scale=out_scale[:, c * P : (c + 1) * P],
+                rhs=hid_code[:, place_halves[h]].bitcast(FP8X4), rhs_scale=hid_scale[:, place_halves[h]],
             )
+        for c in range(OUT_TILES):
+            nc.tensor.matmul_mx(
+                out=q_acc[c][:], start=True, stop=True,
+                lhsT=wo_sb[:, c * P : (c + 1) * P].bitcast(FP8X4), lhsT_scale=out_scale[:, N + c * P : N + (c + 1) * P],
+                rhs=hid_code[:].bitcast(FP8X4), rhs_scale=hid_scale[:],
+            )
+
+        def board_at(c, h):
+            return boards[c][:].indirect(entries(board_list, place_halves[h].start, place_halves[h].stop))
+
         nc.scalar.copy(out=p_sb[0, 0][:], in_=p_acc[0, 0][:])
-        nc.scalar.activation(out=boards[0][:].indirect(board_list[:, span_cols[0]]), in_=p_sb[0, 0][:], func=COPY)
+        nc.scalar.activation(out=board_at(0, 0), in_=p_sb[0, 0][:], func=COPY)
         for c, h in ((1, 0), (1, 1), (0, 1)):
             nc.vector.tensor_copy(out=p_sb[c, h][:], in_=p_acc[c, h][:])
-        for c, h in ((1, 0), (1, 1), (0, 1)):
-            nc.vector.tensor_copy(out=boards[c][:].indirect(board_list[:, span_cols[h]]), in_=p_sb[c, h][:])
-        for c in range(2):
+            nc.vector.tensor_copy(out=board_at(c, h), in_=p_sb[c, h][:])
+        for c in range(OUT_TILES):
             nc.scalar.copy(out=q_sb[c][:], in_=q_acc[c][:])
 
-        left = [new("left%d" % c, [P, E], F32) for c in range(2)]
-        right = [new("right%d" % c, [P, E], F32) for c in range(2)]
-        best = [new("best%d" % c, [P, E], F32) for c in range(2)]
-        for c in range(2):
-            nc.scalar.activation(out=right[c][:], in_=q_sb[c][:].indirect(second_list[:]), func=COPY, scale=sp_sb[:, c : c + 1])
-        for c in (1, 0):
-            nc.scalar.activation(out=left[c][:], in_=boards[c][:].indirect(first_list[:]), func=COPY, scale=so_sb[:, c : c + 1])
-            nc.vector.tensor_tensor(out=best[c][:], in0=left[c][:], in1=right[c][:], op=MAX)
+        from_board = [new("from_board%d" % c, [P, E], F32) for c in range(OUT_TILES)]
+        from_q = [new("from_q%d" % c, [P, E], F32) for c in range(OUT_TILES)]
+        best = [new("best%d" % c, [P, E], F32) for c in range(OUT_TILES)]
+        for c in range(OUT_TILES):
+            fetch(from_q[c][:], q_sb[c], second_list[:], sp_sb[:, c : c + 1])
+        for c in reversed(range(OUT_TILES)):
+            fetch(from_board[c][:], boards[c], first_list[:], so_sb[:, c : c + 1])
+            nc.vector.tensor_tensor(out=best[c][:], in0=from_board[c][:], in1=from_q[c][:], op=MAX)
             nc.sync.dma_start(out=out[c * P : (c + 1) * P, :], in_=best[c][:])

from contextlib import ExitStack

import concourse.mybir as mybir

K, J, R, T, Z, M, O, N, E, G = 512, 512, 512, 1024, 512, 1024, 256, 256, 128, 512
FLOPS = 2 * (K * R * J + Z * R * J + 2 * R * N * O)

F32 = mybir.dt.float32
BF16 = mybir.dt.bfloat16
I32 = mybir.dt.int32
U32 = mybir.dt.uint32
U16 = mybir.dt.uint16
U8 = mybir.dt.uint8
FP8X4 = mybir.dt.float8_e4m3fn_x4
FP4X4 = mybir.dt.float4_e2m1fn_x4
COPY = mybir.ActivationFunctionType.Copy
RELU = mybir.ActivationFunctionType.Relu
ADD = mybir.AluOpType.add
MAX = mybir.AluOpType.max

P = 128
PACK = 4
QUAD = 32
QUADS = P // QUAD
ROWS = 4
PER_COL = 16
LINE = 16
WORD = 4
W_SCALE_AT = 4
W_STAGE_AT = 64
SLOT_HALF = J // 2
PLACE_HALF = O // 2
OUT_TILES = N // P


def tile_picked_basedetail_plain_bank_kept_outcomes_outboard_kernel(
    tc, ta, tb, ga, gb, w_words, w_scales, xo_words, xo_scales, w2_words, w2_scales, sa,
    wb_words, wb_scales, wo_words, wo_scales, so, sp,
    offs, offs2, offs3, offs4, offs5, offs6, offs7, out,
):
    nc = tc.nc
    with ExitStack() as ctx:
        lists = ctx.enter_context(tc.tile_pool(name="lists", bufs=1))
        sb = ctx.enter_context(tc.tile_pool(name="sb", bufs=1))
        psum = ctx.enter_context(tc.psum_pool(name="psum", bufs=1))

        def new(name, shape, dtype):
            return sb.tile(shape, dtype, name=name, align_bytes=64)

        def load_list(name, src):
            tile = lists.tile(list(src.shape), U16, name=name)
            nc.sync.dma_start(tile[:], src)
            return tile

        def load_fp8_words(name, src):
            tile = new(name, [P, src.shape[2]], U32)
            nc.sync.dma_start(out=tile[:].bitcast(I32), in_=src[0].rearrange("p c b -> p (c b)").bitcast(I32))
            return tile

        def load_fp4_words(name, src):
            tile = new(name, [P, src.shape[2]], U8)
            nc.sync.dma_start(out=tile[:].bitcast(I32), in_=src[0].bitcast(I32))
            return tile

        def load_plane(name, table, t):
            tile = new(name, [P, T], F32)
            nc.sync.dma_start(out=tile[:], in_=table.rearrange("(p t) c -> p t c", t=PACK)[:, t, :])
            return tile

        def load_by_plane(queue, name, vec):
            tile = new(name, [P, PACK], F32)
            queue.dma_start(out=tile[:], in_=vec.rearrange("(p t) o -> p (t o)", t=PACK))
            return tile

        def load_by_tile(name, vec):
            tile = new(name, [P, OUT_TILES], F32)
            with nc.allow_non_contiguous_dma(reason="one float a partition and tile"):
                nc.sync.dma_start(out=tile[:], in_=vec.rearrange("(c p) o -> p (c o)", p=P))
            return tile

        def by_quadrant(scales):
            return scales[0].rearrange("(q r) c -> r q c", r=ROWS).bitcast(I32)

        def deal(src, dst, element_bytes):
            run = LINE // element_bytes
            return dict(
                out=dst.rearrange("p (t c i) -> p c t i", t=PACK, i=run),
                in_=src.rearrange("p (c i t) -> p c t i", t=PACK, i=run),
            )

        def entries(offsets, lo, hi):
            return offsets[:, lo // PER_COL : hi // PER_COL]

        def fetch(dst, window, offsets, scale):
            nc.scalar.activation(out=dst, in_=window[:].indirect(offsets), func=COPY, scale=scale)

        xo_stage = new("xo_stage", [ROWS, QUADS, M // WORD], I32)
        nc.gpsimd.dma_start(out=xo_stage[:], in_=by_quadrant(xo_scales))
        w_stage = new("w_stage", [P, QUADS, R // WORD], I32)
        nc.vector.memset(w_stage[W_STAGE_AT : W_STAGE_AT + QUAD], 0)
        nc.gpsimd.dma_start(out=w_stage[W_STAGE_AT : W_STAGE_AT + ROWS], in_=by_quadrant(w2_scales))
        xo_rows = new("xo_rows", [P, M], U8)
        nc.vector.memset(xo_rows[:].bitcast(I32), 0)
        out_scale = new("out_scale", [P, 2 * N], U8)
        nc.vector.memset(out_scale[:].bitcast(I32), 0)
        boards = [new("board%d" % c, [P, G], F32) for c in range(OUT_TILES)]
        for board in boards:
            nc.vector.memset(board[:], 0.0)

        def load_scale_rows(cols, scales):
            for q in range(QUADS):
                nc.sync.dma_start(
                    out=out_scale[QUAD * q : QUAD * q + ROWS, cols].bitcast(I32),
                    in_=scales[0][ROWS * q : ROWS * (q + 1), :].bitcast(I32),
                )

        ta_sb, tb_sb = [], []
        tb_sb.append(load_plane("tb0", tb, 0))
        gb_sb = load_by_plane(nc.scalar, "gb_sb", gb)
        ga_sb = load_by_plane(nc.scalar, "ga_sb", ga)
        detail_list = load_list("detail_list", offs2)
        ta_sb.append(load_plane("ta0", ta, 0))
        base_list = load_list("base_list", offs)
        note_list = load_list("note_list", offs3)
        tb_sb.append(load_plane("tb1", tb, 1))
        w_rows_at = W_STAGE_AT + W_SCALE_AT
        nc.sync.dma_start(out=w_stage[w_rows_at : w_rows_at + ROWS], in_=by_quadrant(w_scales))
        xo_sb = load_fp8_words("xo_sb", xo_words)
        ta_sb.append(load_plane("ta1", ta, 1))
        tb_sb.append(load_plane("tb2", tb, 2))
        ta_sb.append(load_plane("ta2", ta, 2))
        tb_sb.append(load_plane("tb3", tb, 3))
        w2_sb = load_fp4_words("w2_sb", w2_words)
        ta_sb.append(load_plane("ta3", ta, 3))
        w_sb = load_fp8_words("w_sb", w_words)
        slot_list = load_list("slot_list", offs4)
        sa_sb = load_by_plane(nc.sync, "sa_sb", sa)
        wb_sb = load_fp4_words("wb_sb", wb_words)
        load_scale_rows(slice(0, N), wb_scales)
        wo_sb = load_fp8_words("wo_sb", wo_words)
        load_scale_rows(slice(N, 2 * N), wo_scales)
        board_list = load_list("board_list", offs5)
        second_list = load_list("second_list", offs7)
        sp_sb = load_by_tile("sp_sb", sp)
        first_list = load_list("first_list", offs6)
        so_sb = load_by_tile("so_sb", so)

        w_rows = new("w_rows", [P, R], U8)
        for q in range(QUADS):
            nc.vector.tensor_copy(out=xo_rows[QUAD * q : QUAD * q + ROWS, :].bitcast(I32), in_=xo_stage[:, q, :])
        xo_scale = new("xo_scale", [P, J], U8)
        nc.vector.tensor_copy(out=xo_scale[:], in_=xo_rows[:].indirect(note_list[:]))
        for q in range(QUADS):
            nc.vector.tensor_copy(
                out=w_rows[QUAD * q : QUAD * (q + 1), :].bitcast(I32), in_=w_stage[W_STAGE_AT : W_STAGE_AT + QUAD, q, :]
            )
        a_scale = new("a_scale", [P, R], U8)
        nc.vector.tensor_copy(**deal(w_rows[:], a_scale[:], 1))

        slot_halves = [slice(h * SLOT_HALF, (h + 1) * SLOT_HALF) for h in range(2)]
        last_pieces = [(0, SLOT_HALF // 2), (SLOT_HALF // 2, SLOT_HALF), (SLOT_HALF, J)]
        detail = [new("detail%d" % u, [P, 2, J], F32) for u in range(2)]
        base = [new("base%d" % u, [P, 2, J], F32) for u in range(2)]
        xo_code = new("xo_code", [P, J], U32)
        w2_code = new("w2_code", [P, 2 * R], U8)
        xc_bf = [new("xc_bf%d" % h, [P, SLOT_HALF, PACK], BF16) for h in range(2)]
        xc_code = [new("xc_code%d" % h, [P, SLOT_HALF], U32) for h in range(2)]
        xc_scale = [new("xc_scale%d" % h, [P, SLOT_HALF], U8) for h in range(2)]

        def fetch_plane(t, pieces):
            u, s = divmod(t, 2)
            fetch(detail[u][:, s, :], tb_sb[t], detail_list[:], gb_sb[:, t : t + 1])
            for lo, hi in pieces:
                fetch(base[u][:, s, lo:hi], ta_sb[t], entries(base_list, lo, hi), ga_sb[:, t : t + 1])

        def add_pair(u, lo, hi):
            h = lo // SLOT_HALF
            nc.vector.tensor_tensor(
                out=xc_bf[h][:, lo - h * SLOT_HALF : hi - h * SLOT_HALF, 2 * u : 2 * u + 2],
                in0=base[u][:, :, lo:hi].rearrange("p s j -> p j s"),
                in1=detail[u][:, :, lo:hi].rearrange("p s j -> p j s"),
                op=ADD,
            )

        nc.vector.tensor_copy(out=xo_code[:], in_=xo_sb[:].indirect(note_list[:]))
        fetch_plane(0, [(0, J)])
        fetch_plane(1, [(0, J)])
        for half in slot_halves:
            add_pair(0, half.start, half.stop)
        nc.vector.tensor_copy(**deal(w2_sb[:].bitcast(U16), w2_code[:].bitcast(U16), 2))
        fetch_plane(2, [(0, J)])
        fetch_plane(3, last_pieces)
        for lo, hi in last_pieces:
            add_pair(1, lo, hi)
        for h in range(2):
            nc.vector.quantize_mx(
                out=xc_code[h][:].bitcast(FP8X4), scales=xc_scale[h][:], in_=xc_bf[h][:].rearrange("p j t -> p (j t)")
            )

        w_code = new("w_code", [P, R], U32)
        nc.scalar.copy(**deal(w_sb[:], w_code[:], WORD))

        kept = [new("kept%d" % t, [P, J], F32) for t in range(PACK)]
        parts = [(t, h) for t in range(PACK) for h in range(2)]
        on_scalar = [(0, 0), (1, 0)]
        a_acc = {}
        for t, h in parts:
            a_acc[t, h] = psum.tile([P, SLOT_HALF], F32, name="bank%d" % (PACK * h + t))
            nc.tensor.matmul_mx(
                out=a_acc[t, h][:], start=True, stop=False,
                lhsT=w2_code[:, 2 * t * P : 2 * (t + 1) * P].bitcast(FP4X4), lhsT_scale=a_scale[:, t * P : (t + 1) * P],
                rhs=xo_code[:, slot_halves[h]].bitcast(FP8X4), rhs_scale=xo_scale[:, slot_halves[h]],
            )
        for t, h in parts:
            nc.tensor.matmul_mx(
                out=a_acc[t, h][:], start=False, stop=True,
                lhsT=w_code[:, t * P : (t + 1) * P].bitcast(FP8X4), lhsT_scale=a_scale[W_SCALE_AT:, t * P : (t + 1) * P],
                rhs=xc_code[h][:].bitcast(FP8X4), rhs_scale=xc_scale[h][:],
            )
            if (t, h) in on_scalar:
                nc.scalar.activation(out=kept[t][:, slot_halves[h]], in_=a_acc[t, h][:], func=RELU)
            else:
                nc.vector.tensor_scalar_max(out=kept[t][:, slot_halves[h]], in0=a_acc[t, h][:], scalar1=0.0)

        place_halves = [slice(h * PLACE_HALF, (h + 1) * PLACE_HALF) for h in range(2)]
        hid_pairs = [new("hid_pair%d" % u, [P, 2, O], BF16) for u in range(2)]
        hid_bf = [new("hid_bf%d" % h, [P, PLACE_HALF, PACK], BF16) for h in range(2)]
        hid_code = new("hid_code", [P, O], U32)
        hid_scale = new("hid_scale", [P, O], U8)

        def fetch_hidden(t, places):
            u, s = divmod(t, 2)
            fetch(hid_pairs[u][:, s, places], kept[t], entries(slot_list, places.start, places.stop), sa_sb[:, t : t + 1])

        def weave_pair(u):
            for h in range(2):
                nc.vector.tensor_copy(
                    out=hid_bf[h][:, :, 2 * u : 2 * u + 2], in_=hid_pairs[u][:, :, place_halves[h]].rearrange("p s o -> p o s")
                )

        fetch_hidden(0, slice(0, O))
        fetch_hidden(1, slice(0, O))
        weave_pair(0)
        fetch_hidden(2, slice(0, O))
        for half in place_halves:
            fetch_hidden(3, half)
        weave_pair(1)
        for h in range(2):
            nc.vector.quantize_mx(
                out=hid_code[:, place_halves[h]].bitcast(FP8X4), scales=hid_scale[:, place_halves[h]],
                in_=hid_bf[h][:].rearrange("p o t -> p (o t)"),
            )

        p_parts = [(c, h) for h in range(2) for c in range(OUT_TILES)]
        p_acc = {(c, h): psum.tile([P, PLACE_HALF], F32, name="bank%d" % (OUT_TILES * h + c)) for c, h in p_parts}
        q_acc = [psum.tile([P, O], F32, name="bank%d" % (len(p_parts) + c)) for c in range(OUT_TILES)]
        p_sb = {(c, h): new("p_sb%d%d" % (c, h), [P, PLACE_HALF], F32) for c, h in p_parts}
        q_sb = [new("q_sb%d" % c, [P, O], F32) for c in range(OUT_TILES)]
        for c, h in p_parts:
            nc.tensor.matmul_mx(
                out=p_acc[c, h][:], start=True, stop=True,
                lhsT=wb_sb[:, 2 * c * P : 2 * (c + 1) * P].bitcast(FP4X4), lhsT_scale=out_scale[:, c * P : (c + 1) * P],
                rhs=hid_code[:, place_halves[h]].bitcast(FP8X4), rhs_scale=hid_scale[:, place_halves[h]],
            )
        for c in range(OUT_TILES):
            nc.tensor.matmul_mx(
                out=q_acc[c][:], start=True, stop=True,
                lhsT=wo_sb[:, c * P : (c + 1) * P].bitcast(FP8X4), lhsT_scale=out_scale[:, N + c * P : N + (c + 1) * P],
                rhs=hid_code[:].bitcast(FP8X4), rhs_scale=hid_scale[:],
            )

        def board_at(c, h):
            return boards[c][:].indirect(entries(board_list, place_halves[h].start, place_halves[h].stop))

        nc.scalar.copy(out=p_sb[0, 0][:], in_=p_acc[0, 0][:])
        nc.scalar.activation(out=board_at(0, 0), in_=p_sb[0, 0][:], func=COPY)
        for c, h in ((1, 0), (1, 1), (0, 1)):
            nc.vector.tensor_copy(out=p_sb[c, h][:], in_=p_acc[c, h][:])
            nc.vector.tensor_copy(out=board_at(c, h), in_=p_sb[c, h][:])
        for c in range(OUT_TILES):
            nc.scalar.copy(out=q_sb[c][:], in_=q_acc[c][:])

        from_board = [new("from_board%d" % c, [P, E], F32) for c in range(OUT_TILES)]
        from_q = [new("from_q%d" % c, [P, E], F32) for c in range(OUT_TILES)]
        best = [new("best%d" % c, [P, E], F32) for c in range(OUT_TILES)]
        for c in range(OUT_TILES):
            fetch(from_q[c][:], q_sb[c], second_list[:], sp_sb[:, c : c + 1])
        for c in reversed(range(OUT_TILES)):
            fetch(from_board[c][:], boards[c], first_list[:], so_sb[:, c : c + 1])
            nc.vector.tensor_tensor(out=best[c][:], in0=from_board[c][:], in1=from_q[c][:], op=MAX)
            nc.sync.dma_start(out=out[c * P : (c + 1) * P, :], in_=best[c][:])
